import numpy as np
import ml_dtypes


def mxq(x, axis, fmt="e4m3"):
    dtype, down = {"e4m3": (ml_dtypes.float8_e4m3fn, 7), "e5m2": (ml_dtypes.float8_e5m2, 14)}[fmt]
    v = np.moveaxis(np.asarray(x, np.float32).astype(ml_dtypes.bfloat16).astype(np.float64), axis, -1)
    blocks = v.reshape(v.shape[:-1] + (-1, 32))
    amax = np.abs(blocks).max(-1, keepdims=True)
    byte = np.maximum(np.where(amax > 0, np.frexp(amax)[1] - 1 + 127, 0) - down, 1)
    scale = np.exp2(byte - 127.0)
    codes = (blocks / scale).astype(np.float32).astype(dtype).astype(np.float64)
    return np.moveaxis((codes * scale).reshape(v.shape), -1, axis)


WIDE = False


def mx_kscale(k):
    if not WIDE:
        return np.ones(k)
    levels = np.array([10, -10, 5, -5, 0])
    if k % 512:
        return np.exp2(np.random.permutation(np.resize(levels, k // 32))).repeat(32)
    a = np.empty((k // 512, 16))
    for p in range(k // 512):
        a[p, :8] = np.random.permutation(np.resize(levels, 8))
        for g in range(8):
            far = levels[np.abs(levels - a[p, g]) >= 10]
            a[p, g + 8] = far[np.random.randint(len(far))]
    return np.exp2(a.ravel()).repeat(32)


def f64(x):
    return np.asarray(x).astype(np.float64)


def striped(idx):
    return np.tile(idx.reshape(-1, 16).T, (8, 1)).astype(np.uint16)


def unstriped(offs):
    return offs[:16].T.reshape(-1).astype(np.int64)


def striped8(idx):
    return np.concatenate([x.reshape(-1, 16).T for x in idx]).astype(np.uint16)


def runs(offs, k):
    lists = np.stack([offs[16 * r : 16 * r + 16].T.reshape(-1) for r in range(8)]).astype(np.int64)
    return lists[np.arange(k) % 512 // 64]


def pack_weight(w):
    k, n = w.shape
    w = f64(np.asarray(w, np.float32).astype(ml_dtypes.bfloat16)).reshape(k // 32, 32, n)
    amax = np.abs(w).max(1)
    byte = np.clip(np.where(amax > 0, np.frexp(amax)[1] - 1 + 127 - 7, 1), 1, 254)
    scaled = (w * np.exp2(127.0 - byte)[:, None, :]).reshape(k, n).astype(np.float32)
    words = np.ascontiguousarray(scaled.reshape(k // 512, 128, 4, n).transpose(0, 1, 3, 2)).astype(ml_dtypes.float8_e4m3fn).view(np.uint8)
    return words, np.ascontiguousarray(byte.astype(np.uint8).reshape(k // 512, 16, n))


def unpack_weight(words, scales):
    g, p, n, _ = words.shape
    vals = np.ascontiguousarray(words).view(ml_dtypes.float8_e4m3fn).astype(np.float64) * np.repeat(np.exp2(scales.astype(np.float64) - 127.0), 8, axis=1)[..., None]
    return vals.transpose(0, 1, 3, 2).reshape(g * 512, n)


def relu(v):
    return np.maximum(v, 0.0)


def sigmoid(v):
    return 1.0 / (1.0 + np.exp(-np.maximum(v, -700.0)))


K, T, S, H, G, U = 512, 2048, 256, 512, 2048, 1024


def setup_inputs():
    n = np.random.standard_normal
    s = mx_kscale(K)[:, None]
    packed_xT = pack_weight(n((K, T)) * s)
    packed_dT = pack_weight(n((K, G)) / s)
    return {
        "x_words": packed_xT[0],
        "x_scales": packed_xT[1],
        "w1": (n((K, H)) / np.sqrt(K) / s).astype(np.float32),
        "sl": np.random.uniform(1.0, 2.0, (H, 1)).astype(np.float32),
        "th": (0.5 * n((H, 1))).astype(np.float32),
        "gs": (np.random.uniform(0.5, 1.5, (K, 1)) * s).astype(np.float32),
        "d_words": packed_dT[0],
        "d_scales": packed_dT[1],
        "offs": striped8(np.random.randint(0, T, (8, S))),
        "n1": striped(np.random.permutation(S)),
        "n2": striped(np.random.permutation(S)),
        "k1": striped8(np.random.randint(0, G, (8, H))),
        "n3": striped(np.random.permutation(U)[:S]),
        "n4": striped(np.random.permutation(S)),
    }


def reference(x_words, x_scales, w1, sl, th, gs, d_words, d_scales, offs, n1, n2, k1, n3, n4):
    d_k1 = unpack_weight(d_words, d_scales)[np.arange(K)[:, None], runs(k1, K)]
    xq = unpack_weight(x_words, x_scales)[np.arange(K)[:, None], runs(offs, K)]
    y = mxq(f64(w1), 0, "e4m3").T @ xq
    ds = np.zeros((H, S))
    ds[:, unstriped(n1)] = y
    sg = sigmoid(f64(sl) * (ds[:, unstriped(n2)] - f64(th)))
    z = f64(gs) * (y * sg)
    h = 0.0625 * ((d_k1.T @ mxq(z, 0, "e4m3")))
    nw = h - (relu(h[:, unstriped(n4)]))
    out = np.zeros((H, U))
    out[:, unstriped(n3)] = nw
    return out

@@ -1,0 +1,179 @@
+from contextlib import ExitStack
+
+import concourse.mybir as mybir
+
+F32 = mybir.dt.float32
+BF16 = mybir.dt.bfloat16
+I32 = mybir.dt.int32
+U32 = mybir.dt.uint32
+U16 = mybir.dt.uint16
+U8 = mybir.dt.uint8
+FP8X4 = mybir.dt.float8_e4m3fn_x4
+ACT = mybir.ActivationFunctionType
+ALU = mybir.AluOpType
+
+P = 128
+PACK = 4
+K, T, S, H, G, U = 512, 2048, 256, 512, 2048, 1024
+WIN = 2 * S
+FLOPS = 2 * K * H * S + 2 * K * H * S
+
+
+def tile_picked_hdenseerlpagez_none_p_kernel(tc, x_words, x_scales, w1, sl, th, gs, d_words, d_scales, offs, n1, n2, k1, n3, n4, out):
+    nc = tc.nc
+    with ExitStack() as ctx:
+        lists = ctx.enter_context(tc.tile_pool(name="lists", bufs=1))
+        keep = ctx.enter_context(tc.tile_pool(name="keep", bufs=1))
+        psum = ctx.enter_context(tc.psum_pool(name="psum", bufs=1))
+
+        def load_list(name, src, entries):
+            tile = lists.tile([P, entries // 16], U16, name=name)
+            nc.sync.dma_start(tile[:], src)
+            return tile
+
+        def load_words(name, tag, src):
+            tile = keep.tile([P, T], U32, name=name, tag=tag, align_bytes=64)
+            nc.sync.dma_start(tile[:].bitcast(I32), src[0].rearrange("p n t -> p (n t)").bitcast(I32))
+            return tile
+
+        def load_scale_rows(name, tag, src, queue):
+            tile = keep.tile([P, T], U8, name=name, tag=tag, align_bytes=64)
+            rows = src[0].bitcast(I32)
+            queue.dma_start(tile[:].bitcast(I32), rows.unsqueeze(1).to_broadcast([16, 8, T // 4]))
+            return tile
+
+        def pick_scales(name, table, offsets, entries, queue):
+            picked = keep.tile([P, entries], U8, name=name + "_picked", align_bytes=64)
+            nc.vector.tensor_copy(picked[:], table[:].indirect(offsets[:]))
+            plane = keep.tile([P, entries], U8, name=name + "_plane", align_bytes=64)
+            nc.vector.tensor_copy(plane[:].bitcast(I32), picked[:].bitcast(I32))
+            for r in range(1, 4):
+                queue.dma_start(plane[:].bitcast(I32)[r:P:32, :], picked[:].bitcast(I32)[8 * r:P:32, :])
+            return plane
+
+        def load_rows(name, src):
+            tile = keep.tile([P, PACK], F32, name=name)
+            nc.gpsimd.dma_start(tile[:], src.rearrange("(p t) o -> p (t o)", t=PACK))
+            return tile
+
+        xs_table = load_scale_rows("xs_table", "slot_c", x_scales, nc.sync)
+        offs_t = load_list("offs_t", offs, S)
+        w_raw = keep.tile([P, PACK, H], F32, name="w_raw", tag="slot_a", align_bytes=64)
+        w_rows = w1.rearrange("(p j) c -> p j c", j=PACK)
+        nc.sync.dma_start(w_raw[:], w_rows)
+        n1_t = load_list("n1_t", n1, S)
+        xw_table = load_words("xw_table", "slot_b", x_words)
+        n2_t = load_list("n2_t", n2, S)
+        k1_t = load_list("k1_t", k1, H)
+        n4_t = load_list("n4_t", n4, S)
+        n3_t = load_list("n3_t", n3, S)
+        sl_t = load_rows("sl_t", sl)
+        th_t = load_rows("th_t", th)
+        gs_t = load_rows("gs_t", gs)
+
+        def clear_page(b, tag):
+            page = keep.tile([P, U], F32, name=f"page{b}", tag=tag, align_bytes=64)
+            nc.vector.memset(page[:].bitcast(I32), 0)
+            return page
+
+        pages = [clear_page(0, "page0"), clear_page(1, "page1")]
+
+        x_plane = pick_scales("xs", xs_table, offs_t, S, nc.scalar)
+
+        w_src = w_raw[:].rearrange("p j (m t) -> p m j t", t=PACK)
+        w_bf = keep.tile([P, PACK * H], BF16, name="w_bf", tag="slot_c", align_bytes=64)
+        w_dst = w_bf[:].rearrange("p (t m j) -> p m j t", t=PACK, j=PACK)
+        nc.vector.tensor_copy(w_dst, w_src)
+        w_codes = keep.tile([P, H], U32, name="w_codes", tag="w_codes", align_bytes=64)
+        w_plane = keep.tile([P, H], U8, name="w_plane", align_bytes=64)
+        nc.vector.quantize_mx(out=w_codes[:].bitcast(FP8X4), scales=w_plane[:], in_=w_bf[:])
+
+        x_codes = keep.tile([P, S], U32, name="x_codes", tag="slot_c", align_bytes=64)
+        nc.vector.tensor_copy(x_codes[:], xw_table[:].indirect(offs_t[:]))
+
+        y = []
+        for t in range(PACK):
+            cols = slice(P * t, P * (t + 1))
+            acc = psum.tile([P, S], F32, name=f"y_acc{t}")
+            nc.tensor.matmul_mx(out=acc[:], lhsT=w_codes[:, cols].bitcast(FP8X4), lhsT_scale=w_plane[:, cols],
+                                rhs=x_codes[:].bitcast(FP8X4), rhs_scale=x_plane[:], start=True, stop=True)
+            y_t = keep.tile([P, S], F32, name=f"y{t}")
+            nc.vector.tensor_copy(y_t[:], acc[:])
+            y.append(y_t)
+
+        pages.append(clear_page(2, "w_codes"))
+        pages.append(clear_page(3, "slot_c"))
+        sl_th = keep.tile([P, PACK], F32, name="sl_th")
+        nc.gpsimd.tensor_tensor(sl_th[:], sl_t[:], th_t[:], ALU.mult)
+        bias = keep.tile([P, PACK], F32, name="bias")
+        nc.gpsimd.tensor_scalar(bias[:], sl_th[:], -1.0, 0.0, ALU.mult, ALU.add)
+
+        dw_table = load_words("dw_table", "slot_a", d_words)
+        ds_table = keep.tile([P, G], U8, name="ds_table", tag="slot_b", align_bytes=64)
+        nc.vector.memset(ds_table[:].bitcast(I32), 0)
+        nc.sync.dma_start(ds_table[:].bitcast(I32)[0:P:8, :], d_scales[0].bitcast(I32))
+        d_plane = pick_scales("ds", ds_table, k1_t, H, nc.sync)
+        d_codes = keep.tile([P, H], U32, name="d_codes", align_bytes=64)
+        nc.vector.tensor_copy(d_codes[:], dw_table[:].indirect(k1_t[:]))
+
+        z_bf = keep.tile([P, S, PACK], BF16, name="z_bf", tag="slot_b", align_bytes=64)
+        sent = [keep.tile([P, WIN], F32, name=f"sent{t}") for t in range(PACK)]
+        sg = [keep.tile([P, S], F32, name=f"sg{t}") for t in range(PACK)]
+        z_codes = keep.tile([P, S], U32, name="z_codes", align_bytes=64)
+        z_plane = keep.tile([P, S], U8, name="z_plane", align_bytes=64)
+        halves = [slice(0, S // 2), slice(S // 2, S)]
+
+        def send(t):
+            nc.scalar.activation(sent[t][:].indirect(n1_t[:]), y[t][:], ACT.Copy)
+
+        def gate(t, places):
+            entries = n2_t[:, places.start // 16:places.stop // 16]
+            nc.scalar.activation(sg[t][:, places], sent[t][:].indirect(entries), ACT.Sigmoid,
+                                 bias=bias[:, t:t + 1], scale=sl_t[:, t:t + 1])
+            nc.vector.scalar_tensor_tensor(z_bf[:, places, t], sg[t][:, places], gs_t[:, t:t + 1], y[t][:, places],
+                                           ALU.mult, ALU.mult)
+
+        def product2(b, places, acc, pos):
+            cols = slice(P * b, P * (b + 1))
+            nc.tensor.matmul_mx(out=acc, lhsT=d_codes[:, cols].bitcast(FP8X4), lhsT_scale=d_plane[:, cols],
+                                rhs=z_codes[:, places].bitcast(FP8X4), rhs_scale=z_plane[:, places],
+                                start=True, stop=True)
+            nc.vector.tensor_scalar(pos[:, places], acc, 0.0625, 0.0, ALU.mult, ALU.max)
+
+        send(0)
+        for t in range(1, PACK):
+            send(t)
+            if t < PACK - 1:
+                gate(t - 1, slice(0, S))
+        pos = [keep.tile([P, WIN], F32, name=f"pos{b}") for b in range(PACK)]
+        parts = [[] for b in range(PACK)]
+        for i, places in enumerate(halves):
+            gate(PACK - 2, places)
+            gate(PACK - 1, places)
+            nc.vector.quantize_mx(out=z_codes[:, places].bitcast(FP8X4), scales=z_plane[:, places],
+                                  in_=z_bf[:, places, :].rearrange("p s t -> p (s t)"))
+            acc = psum.tile([P, S // 2], F32, name=f"h0_acc{i}", tag=f"y_acc{i}")
+            product2(0, places, acc[:], pos[0])
+            parts[0].append((places, acc))
+        for b in range(1, PACK):
+            acc = psum.tile([P, S], F32, name=f"h_acc{b}")
+            product2(b, slice(0, S), acc[:], pos[b])
+            parts[b].append((slice(0, S), acc))
+
+        nw = [keep.tile([P, S], F32, name=f"nw{b}") for b in range(PACK)]
+
+        def fetch(b):
+            got = keep.tile([P, S], F32, name=f"got{b}")
+            nc.scalar.activation(got[:], pos[b][:].indirect(n4_t[:]), ACT.Copy)
+            for places, acc in parts[b]:
+                nc.vector.scalar_tensor_tensor(nw[b][:, places], acc[:], 0.0625, got[:, places], ALU.mult, ALU.subtract)
+
+        def put(b):
+            nc.scalar.activation(pages[b][:].indirect(n3_t[:]), nw[b][:], ACT.Copy)
+            nc.sync.dma_start(out[P * b:P * (b + 1), :], pages[b][:])
+
+        fetch(0)
+        for b in range(1, PACK):
+            fetch(b)
+            put(b - 1)
+        put(PACK - 1)

@@ -57,6 +57,9 @@ def tile_picked_hdenseerlpagez_none_p_kernel(tc, x_words, x_scales, w1, sl, th, 
             return tile
 
         xs_table = load_scale_rows("xs_table", "slot_c", x_scales, nc.sync)
+        warm = keep.tile([P, 2], F32, name="warm")
+        nc.vector.memset(warm[:, 0:1], 0.0)
+        nc.scalar.activation(warm[:, 1:2], warm[:, 0:1], ACT.Sigmoid)
         offs_t = load_list("offs_t", offs, S)
         w_raw = keep.tile([P, PACK, H], F32, name="w_raw", tag="slot_a", align_bytes=64)
         w_rows = w1.rearrange("(p j) c -> p j c", j=PACK)

@@ -83,9 +83,9 @@ def tile_picked_hdenseerlpagez_none_p_kernel(tc, x_words, x_scales, w1, sl, th, 
 
         x_plane = pick_scales("xs", xs_table, offs_t, S, nc.scalar)
 
-        w_src = w_raw[:].rearrange("p j (m t) -> p m j t", t=PACK)
+        w_src = w_raw[:].rearrange("p j (m t) -> p m t j", t=PACK)
         w_bf = keep.tile([P, PACK * H], BF16, name="w_bf", tag="slot_c", align_bytes=64)
-        w_dst = w_bf[:].rearrange("p (t m j) -> p m j t", t=PACK, j=PACK)
+        w_dst = w_bf[:].rearrange("p (t m j) -> p m t j", t=PACK, j=PACK)
         nc.vector.tensor_copy(w_dst, w_src)
         w_codes = keep.tile([P, H], U32, name="w_codes", tag="w_codes", align_bytes=64)
         w_plane = keep.tile([P, H], U8, name="w_plane", align_bytes=64)
@@ -144,14 +144,15 @@ def tile_picked_hdenseerlpagez_none_p_kernel(tc, x_words, x_scales, w1, sl, th, 
             nc.vector.tensor_scalar(pos[:, places], acc, 0.0625, 0.0, ALU.mult, ALU.max)
 
         send(0)
-        for t in range(1, PACK):
+        for t in range(1, PACK - 1):
             send(t)
-            if t < PACK - 1:
-                gate(t - 1, slice(0, S))
+            gate(t - 1, slice(0, S))
+        gate(PACK - 2, halves[0])
+        send(PACK - 1)
+        gate(PACK - 2, halves[1])
         pos = [keep.tile([P, WIN], F32, name=f"pos{b}") for b in range(PACK)]
         parts = [[] for b in range(PACK)]
         for i, places in enumerate(halves):
-            gate(PACK - 2, places)
             gate(PACK - 1, places)
             nc.vector.quantize_mx(out=z_codes[:, places].bitcast(FP8X4), scales=z_plane[:, places],
                                   in_=z_bf[:, places, :].rearrange("p s t -> p (s t)"))

from contextlib import ExitStack

import concourse.mybir as mybir

F32 = mybir.dt.float32
BF16 = mybir.dt.bfloat16
I32 = mybir.dt.int32
U32 = mybir.dt.uint32
U16 = mybir.dt.uint16
U8 = mybir.dt.uint8
FP8X4 = mybir.dt.float8_e4m3fn_x4
ACT = mybir.ActivationFunctionType
ALU = mybir.AluOpType

P = 128
PACK = 4
K, T, S, H, G, U = 512, 2048, 256, 512, 2048, 1024
WIN = 2 * S
FLOPS = 2 * K * H * S + 2 * K * H * S


def tile_picked_hdenseerlpagez_none_p_kernel(tc, x_words, x_scales, w1, sl, th, gs, d_words, d_scales, offs, n1, n2, k1, n3, n4, out):
    nc = tc.nc
    with ExitStack() as ctx:
        lists = ctx.enter_context(tc.tile_pool(name="lists", bufs=1))
        keep = ctx.enter_context(tc.tile_pool(name="keep", bufs=1))
        psum = ctx.enter_context(tc.psum_pool(name="psum", bufs=1))

        def load_list(name, src, entries):
            tile = lists.tile([P, entries // 16], U16, name=name)
            nc.sync.dma_start(tile[:], src)
            return tile

        def load_words(name, tag, src):
            tile = keep.tile([P, T], U32, name=name, tag=tag, align_bytes=64)
            nc.sync.dma_start(tile[:].bitcast(I32), src[0].rearrange("p n t -> p (n t)").bitcast(I32))
            return tile

        def load_scale_rows(name, tag, src, queue):
            tile = keep.tile([P, T], U8, name=name, tag=tag, align_bytes=64)
            rows = src[0].bitcast(I32)
            queue.dma_start(tile[:].bitcast(I32), rows.unsqueeze(1).to_broadcast([16, 8, T // 4]))
            return tile

        def pick_scales(name, table, offsets, entries, queue):
            picked = keep.tile([P, entries], U8, name=name + "_picked", align_bytes=64)
            nc.vector.tensor_copy(picked[:], table[:].indirect(offsets[:]))
            plane = keep.tile([P, entries], U8, name=name + "_plane", align_bytes=64)
            nc.vector.tensor_copy(plane[:].bitcast(I32), picked[:].bitcast(I32))
            for r in range(1, 4):
                queue.dma_start(plane[:].bitcast(I32)[r:P:32, :], picked[:].bitcast(I32)[8 * r:P:32, :])
            return plane

        def load_rows(name, src):
            tile = keep.tile([P, PACK], F32, name=name)
            nc.gpsimd.dma_start(tile[:], src.rearrange("(p t) o -> p (t o)", t=PACK))
            return tile

        xs_table = load_scale_rows("xs_table", "slot_c", x_scales, nc.sync)
        warm = keep.tile([P, 2], F32, name="warm")
        nc.vector.memset(warm[:, 0:1], 0.0)
        nc.scalar.activation(warm[:, 1:2], warm[:, 0:1], ACT.Sigmoid)
        offs_t = load_list("offs_t", offs, S)
        w_raw = keep.tile([P, PACK, H], F32, name="w_raw", tag="slot_a", align_bytes=64)
        w_rows = w1.rearrange("(p j) c -> p j c", j=PACK)
        nc.sync.dma_start(w_raw[:], w_rows)
        n1_t = load_list("n1_t", n1, S)
        xw_table = load_words("xw_table", "slot_b", x_words)
        n2_t = load_list("n2_t", n2, S)
        k1_t = load_list("k1_t", k1, H)
        n4_t = load_list("n4_t", n4, S)
        n3_t = load_list("n3_t", n3, S)
        sl_t = load_rows("sl_t", sl)
        th_t = load_rows("th_t", th)
        gs_t = load_rows("gs_t", gs)

        def clear_page(b, tag):
            page = keep.tile([P, U], F32, name=f"page{b}", tag=tag, align_bytes=64)
            nc.vector.memset(page[:].bitcast(I32), 0)
            return page

        pages = [clear_page(0, "page0"), clear_page(1, "page1")]

        x_plane = pick_scales("xs", xs_table, offs_t, S, nc.scalar)

        w_src = w_raw[:].rearrange("p j (m t) -> p m t j", t=PACK)
        w_bf = keep.tile([P, PACK * H], BF16, name="w_bf", tag="slot_c", align_bytes=64)
        w_dst = w_bf[:].rearrange("p (t m j) -> p m t j", t=PACK, j=PACK)
        nc.vector.tensor_copy(w_dst, w_src)
        w_codes = keep.tile([P, H], U32, name="w_codes", tag="w_codes", align_bytes=64)
        w_plane = keep.tile([P, H], U8, name="w_plane", align_bytes=64)
        nc.vector.quantize_mx(out=w_codes[:].bitcast(FP8X4), scales=w_plane[:], in_=w_bf[:])

        x_codes = keep.tile([P, S], U32, name="x_codes", tag="slot_c", align_bytes=64)
        nc.vector.tensor_copy(x_codes[:], xw_table[:].indirect(offs_t[:]))

        y = []
        for t in range(PACK):
            cols = slice(P * t, P * (t + 1))
            acc = psum.tile([P, S], F32, name=f"y_acc{t}")
            nc.tensor.matmul_mx(out=acc[:], lhsT=w_codes[:, cols].bitcast(FP8X4), lhsT_scale=w_plane[:, cols],
                                rhs=x_codes[:].bitcast(FP8X4), rhs_scale=x_plane[:], start=True, stop=True)
            y_t = keep.tile([P, S], F32, name=f"y{t}")
            nc.vector.tensor_copy(y_t[:], acc[:])
            y.append(y_t)

        pages.append(clear_page(2, "w_codes"))
        pages.append(clear_page(3, "slot_c"))
        sl_th = keep.tile([P, PACK], F32, name="sl_th")
        nc.gpsimd.tensor_tensor(sl_th[:], sl_t[:], th_t[:], ALU.mult)
        bias = keep.tile([P, PACK], F32, name="bias")
        nc.gpsimd.tensor_scalar(bias[:], sl_th[:], -1.0, 0.0, ALU.mult, ALU.add)

        dw_table = load_words("dw_table", "slot_a", d_words)
        ds_table = keep.tile([P, G], U8, name="ds_table", tag="slot_b", align_bytes=64)
        nc.vector.memset(ds_table[:].bitcast(I32), 0)
        nc.sync.dma_start(ds_table[:].bitcast(I32)[0:P:8, :], d_scales[0].bitcast(I32))
        d_plane = pick_scales("ds", ds_table, k1_t, H, nc.sync)
        d_codes = keep.tile([P, H], U32, name="d_codes", align_bytes=64)
        nc.vector.tensor_copy(d_codes[:], dw_table[:].indirect(k1_t[:]))

        z_bf = keep.tile([P, S, PACK], BF16, name="z_bf", tag="slot_b", align_bytes=64)
        sent = [keep.tile([P, WIN], F32, name=f"sent{t}") for t in range(PACK)]
        sg = [keep.tile([P, S], F32, name=f"sg{t}") for t in range(PACK)]
        z_codes = keep.tile([P, S], U32, name="z_codes", align_bytes=64)
        z_plane = keep.tile([P, S], U8, name="z_plane", align_bytes=64)
        halves = [slice(0, S // 2), slice(S // 2, S)]

        def send(t):
            nc.scalar.activation(sent[t][:].indirect(n1_t[:]), y[t][:], ACT.Copy)

        def gate(t, places):
            entries = n2_t[:, places.start // 16:places.stop // 16]
            nc.scalar.activation(sg[t][:, places], sent[t][:].indirect(entries), ACT.Sigmoid,
                                 bias=bias[:, t:t + 1], scale=sl_t[:, t:t + 1])
            nc.vector.scalar_tensor_tensor(z_bf[:, places, t], sg[t][:, places], gs_t[:, t:t + 1], y[t][:, places],
                                           ALU.mult, ALU.mult)

        def product2(b, places, acc, pos):
            cols = slice(P * b, P * (b + 1))
            nc.tensor.matmul_mx(out=acc, lhsT=d_codes[:, cols].bitcast(FP8X4), lhsT_scale=d_plane[:, cols],
                                rhs=z_codes[:, places].bitcast(FP8X4), rhs_scale=z_plane[:, places],
                                start=True, stop=True)
            nc.vector.tensor_scalar(pos[:, places], acc, 0.0625, 0.0, ALU.mult, ALU.max)

        send(0)
        for t in range(1, PACK - 1):
            send(t)
            gate(t - 1, slice(0, S))
        gate(PACK - 2, halves[0])
        send(PACK - 1)
        gate(PACK - 2, halves[1])
        pos = [keep.tile([P, WIN], F32, name=f"pos{b}") for b in range(PACK)]
        parts = [[] for b in range(PACK)]
        for i, places in enumerate(halves):
            gate(PACK - 1, places)
            nc.vector.quantize_mx(out=z_codes[:, places].bitcast(FP8X4), scales=z_plane[:, places],
                                  in_=z_bf[:, places, :].rearrange("p s t -> p (s t)"))
            acc = psum.tile([P, S // 2], F32, name=f"h0_acc{i}", tag=f"y_acc{i}")
            product2(0, places, acc[:], pos[0])
            parts[0].append((places, acc))
        for b in range(1, PACK):
            acc = psum.tile([P, S], F32, name=f"h_acc{b}")
            product2(b, slice(0, S), acc[:], pos[b])
            parts[b].append((slice(0, S), acc))

        nw = [keep.tile([P, S], F32, name=f"nw{b}") for b in range(PACK)]

        def fetch(b):
            got = keep.tile([P, S], F32, name=f"got{b}")
            nc.scalar.activation(got[:], pos[b][:].indirect(n4_t[:]), ACT.Copy)
            for places, acc in parts[b]:
                nc.vector.scalar_tensor_tensor(nw[b][:, places], acc[:], 0.0625, got[:, places], ALU.mult, ALU.subtract)

        def put(b):
            nc.scalar.activation(pages[b][:].indirect(n3_t[:]), nw[b][:], ACT.Copy)
            nc.sync.dma_start(out[P * b:P * (b + 1), :], pages[b][:])

        fetch(0)
        for b in range(1, PACK):
            fetch(b)
            put(b - 1)
        put(PACK - 1)
